import numpy as np
import ml_dtypes


def mxq(x, axis, fmt="e4m3"):
    dtype, down = {"e4m3": (ml_dtypes.float8_e4m3fn, 7), "e5m2": (ml_dtypes.float8_e5m2, 14)}[fmt]
    v = np.moveaxis(np.asarray(x, np.float32).astype(ml_dtypes.bfloat16).astype(np.float64), axis, -1)
    blocks = v.reshape(v.shape[:-1] + (-1, 32))
    amax = np.abs(blocks).max(-1, keepdims=True)
    byte = np.maximum(np.where(amax > 0, np.frexp(amax)[1] - 1 + 127, 0) - down, 1)
    scale = np.exp2(byte - 127.0)
    codes = (blocks / scale).astype(np.float32).astype(dtype).astype(np.float64)
    return np.moveaxis((codes * scale).reshape(v.shape), -1, axis)


WIDE = False


def mx_kscale(k):
    if not WIDE:
        return np.ones(k)
    levels = np.array([10, -10, 5, -5, 0])
    if k % 512:
        return np.exp2(np.random.permutation(np.resize(levels, k // 32))).repeat(32)
    a = np.empty((k // 512, 16))
    for p in range(k // 512):
        a[p, :8] = np.random.permutation(np.resize(levels, 8))
        for g in range(8):
            far = levels[np.abs(levels - a[p, g]) >= 10]
            a[p, g + 8] = far[np.random.randint(len(far))]
    return np.exp2(a.ravel()).repeat(32)


def f64(x):
    return np.asarray(x).astype(np.float64)


def striped(idx):
    return np.tile(idx.reshape(-1, 16).T, (8, 1)).astype(np.uint16)


def unstriped(offs):
    return offs[:16].T.reshape(-1).astype(np.int64)


E2M1 = np.array([0.0, 0.5, 1.0, 1.5, 2.0, 3.0, 4.0, 6.0, -0.0, -0.5, -1.0, -1.5, -2.0, -3.0, -4.0, -6.0])


def pack_weight(w, fmt):
    k, n = w.shape
    w = f64(np.asarray(w, np.float32).astype(ml_dtypes.bfloat16)).reshape(k // 32, 32, n)
    amax = np.abs(w).max(1)
    if fmt == "e4m3":
        byte = np.frexp(amax)[1] - 1 + 127 - 7
    else:
        mant, ex = np.frexp(amax / 6.0)
        byte = np.where(mant > 0.5, ex, ex - 1) + 127
    byte = np.clip(np.where(amax > 0, byte, 1), 1, 254)
    scaled = (w * np.exp2(127.0 - byte)[:, None, :]).reshape(k, n).astype(np.float32)
    by_word = np.ascontiguousarray(scaled.reshape(k // 512, 128, 4, n).transpose(0, 1, 3, 2))
    if fmt == "e4m3":
        words = by_word.astype(ml_dtypes.float8_e4m3fn).view(np.uint8)
    else:
        c = by_word.astype(ml_dtypes.float4_e2m1fn).view(np.uint8) & 0xF
        words = (c[..., 0::2] | (c[..., 1::2] << 4)).reshape(k // 512, 128, 2 * n)
    return np.ascontiguousarray(words), np.ascontiguousarray(byte.astype(np.uint8).reshape(k // 512, 16, n))


def unpack_weight(words, scales, fmt):
    g, _, n = scales.shape
    words = np.ascontiguousarray(words).reshape(g, 128, n, -1)
    if fmt == "e4m3":
        vals = words.view(ml_dtypes.float8_e4m3fn).astype(np.float64)
    else:
        nib = np.empty((g, 128, n, 4), np.uint8)
        nib[..., 0::2] = words & 0xF
        nib[..., 1::2] = words >> 4
        vals = E2M1[nib]
    vals = vals * np.repeat(np.exp2(scales.astype(np.float64) - 127.0), 8, axis=1)[..., None]
    return vals.transpose(0, 1, 3, 2).reshape(g * 512, n)


def gelu(v):
    return 0.5 * v * (1.0 + np.tanh(np.sqrt(2.0 / np.pi) * (v + 0.044715 * v**3)))


K, T, S, H, T2, N = 1024, 4096, 1024, 512, 2048, 384

def setup_inputs():
    n = np.random.standard_normal
    s = mx_kscale(K)[:, None]
    u = mx_kscale(H)[:, None]
    tab_words, tab_scales = pack_weight(n((K, T)) * s, "e4m3")
    w2_words, w2_scales = pack_weight(0.8 * n((K, H)) / np.sqrt(K) / s, "e2m1")
    w3_words, w3_scales = pack_weight(n((K, H)) / np.sqrt(K) / s * u.T, "e4m3")
    return {
        "tab_words": tab_words, "tab_scales": tab_scales,
        "offs": striped(np.random.permutation(T)[:S]),
        "w1": (n((K, H)) / np.sqrt(K) / s).astype(np.float32),
        "w2_words": w2_words, "w2_scales": w2_scales,
        "w3_words": w3_words, "w3_scales": w3_scales,
        "offs2": striped(np.random.permutation(T2)[:S]),
        "wg1": np.exp(0.3 * n((128, S))).astype(np.float32),
        "offs3": striped(np.random.permutation(T2)[:S]),
        "wg2": np.exp(0.3 * n((128, S))).astype(np.float32),
        "prior": (n((H, T2)) * u).astype(np.float32),
        "w4": (n((H, N)) / np.sqrt(H) / u).astype(np.float32),
    }

def reference(tab_words, tab_scales, offs, w1, w2_words, w2_scales, w3_words, w3_scales,
              offs2, wg1, offs3, wg2, prior, w4):
    v = unpack_weight(tab_words, tab_scales, "e4m3")[:, unstriped(offs)]
    b = unpack_weight(w2_words, w2_scales, "e2m1").T @ v
    h1 = (mxq(f64(w1), 0, "e4m3").T @ v) + b * b
    h2 = unpack_weight(w3_words, w3_scales, "e4m3").T @ v
    pageA = np.zeros((H, T2))
    pageA[:, unstriped(offs2)] = np.tile(f64(wg1), (H // 128, 1)) * h1
    pageB = np.zeros((H, T2))
    pageB[:, unstriped(offs3)] = np.tile(f64(wg2), (H // 128, 1)) * h2
    u0 = f64(prior)
    z = u0 + 1.0 / (1.0 + np.exp(-pageA)) * (pageB - u0)
    return mxq(f64(w4), 0, "e4m3").T @ mxq(z, 0, "e4m3")

@@ -1,0 +1,361 @@
+from contextlib import ExitStack
+
+import concourse.mybir as mybir
+from concourse.masks import make_identity
+
+K, T, S, H, T2, N = 1024, 4096, 1024, 512, 2048, 384
+FLOPS = 3 * 2 * K * H * S + 2 * H * N * T2
+
+F32 = mybir.dt.float32
+BF16 = mybir.dt.bfloat16
+I32 = mybir.dt.int32
+U32 = mybir.dt.uint32
+U16 = mybir.dt.uint16
+U8 = mybir.dt.uint8
+FP8X4 = mybir.dt.float8_e4m3fn_x4
+FP4X4 = mybir.dt.float4_e2m1fn_x4
+MULT = mybir.AluOpType.mult
+ADD = mybir.AluOpType.add
+COPY = mybir.ActivationFunctionType.Copy
+SQUARE = mybir.ActivationFunctionType.Square
+SIGMOID = mybir.ActivationFunctionType.Sigmoid
+
+P = 128
+PACK = 4
+BANK = 512
+PASSES = K // (P * PACK)
+SLICES = H // P
+CHUNKS = T2 // BANK
+HALVES = S // BANK
+LIST_COLS = BANK // 16
+
+
+def tile_list_claim_evidence_desk_kernel(
+    tc, tab_words, tab_scales, offs, w1, w2_words, w2_scales, w3_words, w3_scales,
+    offs2, wg1, offs3, wg2, prior, w4, out,
+):
+    nc = tc.nc
+    with ExitStack() as ctx:
+        lists = ctx.enter_context(tc.tile_pool(name="lists", bufs=1))
+        sb = ctx.enter_context(tc.tile_pool(name="sb", bufs=1))
+        ps = ctx.enter_context(tc.psum_pool(name="ps", bufs=1))
+
+        def sbuf(name, cols, dtype, tag=None):
+            return sb.tile([P, cols], dtype, name=name, tag=tag or name, align_bytes=64)
+
+        def span(i, width):
+            return slice(i * width, (i + 1) * width)
+
+        idx = lists.tile([P, S // 16], U16, name="idx")
+        idx2 = lists.tile([P, S // 16], U16, name="idx2")
+        idx3 = lists.tile([P, S // 16], U16, name="idx3")
+
+        diff_banks = [ps.tile([P, BANK], F32, name="diff%d" % g) for g in range(CHUNKS)]
+        lin_banks = [ps.tile([P, BANK], F32, name="lin%d" % h) for h in range(HALVES)]
+        ring_banks = [ps.tile([P, BANK], F32, name="ring%d" % h) for h in range(2)]
+        ring_count = [0]
+
+        def ring_bank():
+            bank = ring_banks[ring_count[0] % 2]
+            ring_count[0] = ring_count[0] + 1
+            return bank
+
+        tab_w = [sbuf("tab_w%d" % a, T, I32, tag="big%d" % a) for a in range(PASSES)]
+        tab_s = sbuf("tab_s", T, U8)
+        got_w = [sbuf("got_w%d" % a, S, U32) for a in range(PASSES)]
+        got_s = sbuf("got_s", S, U8)
+        got_s1 = sbuf("got_s1", S, U8)
+        w1_raw0 = sbuf("w1_raw0", PACK * H, F32, tag="stage0")
+        slot_x = sbuf("slot_x", PACK * H, F32)
+        w1_raw = [w1_raw0, slot_x]
+        w1_bf = sbuf("w1_bf", PASSES * PACK * H, BF16, tag="stage1")
+        w1_c = sbuf("w1_c", PASSES * H, U32)
+        w1_s = sbuf("w1_s", PASSES * H, U8)
+        w2_c = sbuf("w2_c", PASSES * 2 * H, U8)
+        w2_s = sbuf("w2_s", PASSES * H, U8)
+        w3_c = sbuf("w3_c", PASSES * H, I32)
+        w3_s = sbuf("w3_s", H, U8)
+        w4_raw = sbuf("w4_raw", PACK * N, F32)
+        w4_bf = sbuf("w4_bf", PACK * N, BF16)
+        w4_c = sbuf("w4_c", N, U32)
+        w4_s = sbuf("w4_s", N, U8)
+        gain1 = sbuf("gain1", S, F32)
+        gain2 = sbuf("gain2", S, F32)
+        prior_t = [sbuf("prior%d" % c, T2, F32, tag="prior%d" % c) for c in range(SLICES)]
+        page_a = [sbuf("page_a%d" % i, T2, F32) for i in range(2)]
+        page_b = [sbuf("page_b%d" % i, T2, F32) for i in range(2)]
+        gate_t = [sbuf("gate_t%d" % i, T2, F32) for i in range(2)]
+        slot_y = sbuf("slot_y", T2, F32)
+        slot_z = sbuf("slot_z", T2, F32)
+        ident = sbuf("ident", P, F32)
+        z_c = [sbuf("z_c%d" % g, BANK, U32) for g in range(CHUNKS)]
+        z_s = [sbuf("z_s%d" % g, BANK, U8) for g in range(CHUNKS)]
+
+        nc.vector.memset(tab_s[:].bitcast(I32), 0)
+        nc.vector.memset(w3_s[:].bitcast(I32), 0)
+        nc.vector.memset(w2_s[:].bitcast(I32), 0)
+        nc.vector.memset(got_s1[:].bitcast(I32), 0)
+        for page in (page_b[0], page_b[1], page_a[0], page_a[1]):
+            nc.vector.memset(page[:], 0.0)
+
+        nc.sync.dma_start(idx[:], offs)
+        for q in range(4):
+            nc.sync.dma_start(
+                out=tab_s[32 * q : 32 * q + 8, :].bitcast(I32),
+                in_=tab_scales[:, 4 * q : 4 * q + 4, :].bitcast(I32),
+            )
+        for a in range(PASSES):
+            nc.sync.dma_start(out=tab_w[a][:], in_=tab_words[a].rearrange("p n t -> p (n t)").bitcast(I32))
+        nc.sync.dma_start(
+            out=w3_c[:].rearrange("p (a n) -> p a n", a=PASSES),
+            in_=w3_words.rearrange("a p n t -> p a (n t)").bitcast(I32),
+        )
+        for q in range(4):
+            nc.sync.dma_start(
+                out=w3_s[32 * q : 32 * q + 8, :].bitcast(I32),
+                in_=w3_scales[:, 4 * q : 4 * q + 4, :].bitcast(I32),
+            )
+        make_identity(nc, ident[:])
+        for q in range(4):
+            nc.gpsimd.dma_start(
+                out=w2_s[32 * q : 32 * q + 4, :].bitcast(I32).rearrange("r (a n) -> r a n", a=PASSES),
+                in_=w2_scales[:, 4 * q : 4 * q + 4, :].bitcast(I32).rearrange("a r n -> r a n"),
+            )
+        nc.sync.dma_start(out=gain2[:], in_=wg2)
+        nc.sync.dma_start(idx3[:], offs3)
+        for a in range(PASSES):
+            nc.sync.dma_start(
+                out=w1_raw[a][:],
+                in_=w1[span(a, P * PACK), :].rearrange("(p j) n -> p (j n)", j=PACK),
+            )
+        nc.sync.dma_start(
+            out=w2_c[:].bitcast(I32).rearrange("p (a n) -> p a n", a=PASSES),
+            in_=w2_words.rearrange("a p n -> p a n").bitcast(I32),
+        )
+        nc.sync.dma_start(out=gain1[:], in_=wg1)
+        nc.sync.dma_start(idx2[:], offs2)
+        for c in range(SLICES):
+            nc.sync.dma_start(out=prior_t[c][:], in_=prior[span(c, P), :])
+        nc.sync.dma_start(out=w4_raw[:], in_=w4.rearrange("(p j) n -> p (j n)", j=PACK))
+
+        nc.vector.tensor_copy(got_s[:], tab_s[:].indirect(idx[:]))
+        for a in range(PASSES):
+            for h in range(HALVES):
+                nc.vector.tensor_copy(
+                    got_w[a][:, span(h, BANK)],
+                    tab_w[a][:].bitcast(U32).indirect(idx[:, span(h, LIST_COLS)]),
+                )
+        for q in range(4):
+            nc.gpsimd.dma_start(
+                out=got_s1[32 * q : 32 * q + 4, :].bitcast(I32),
+                in_=got_s[32 * q + 4 : 32 * q + 8, :].bitcast(I32),
+            )
+
+        def project(bank, which, c, h):
+            for a in range(PASSES):
+                cols = slice(a * H + c * P, a * H + (c + 1) * P)
+                if which == 1:
+                    lhs, lhs_s, rhs_s = w1_c[:, cols].bitcast(FP8X4), w1_s[:, cols], got_s[4 * a : P, span(h, BANK)]
+                elif which == 2:
+                    lhs = w2_c[:, 2 * cols.start : 2 * cols.stop].bitcast(FP4X4)
+                    lhs_s, rhs_s = w2_s[:, cols], (got_s, got_s1)[a][:, span(h, BANK)]
+                else:
+                    lhs, lhs_s = w3_c[:, cols].bitcast(FP8X4), w3_s[4 * a : P, span(c, P)]
+                    rhs_s = got_s[4 * a : P, span(h, BANK)]
+                nc.tensor.matmul_mx(
+                    out=bank[:], lhsT=lhs, lhsT_scale=lhs_s,
+                    rhs=got_w[a][:, span(h, BANK)].bitcast(FP8X4), rhs_scale=rhs_s,
+                    start=(a == 0), stop=(a == PASSES - 1),
+                )
+
+        def cast_interleave(dst, src):
+            nc.scalar.copy(
+                out=dst.rearrange("p (c i t) -> p c t i", i=4, t=PACK),
+                in_=src.rearrange("p (t c i) -> p c t i", i=4, t=PACK),
+            )
+
+        def evidence_mm(c, banks):
+            for h in range(HALVES):
+                project(banks[h], 3, c, h)
+
+        def evidence_out(banks, dst, h):
+            nc.scalar.activation(dst[:, span(h, BANK)], banks[h][:], COPY, scale=-1.0)
+
+        def scatter(page, offsets, values, gain):
+            nc.vector.tensor_tensor(page[:].indirect(offsets), values, gain, MULT)
+
+        def turn(bank, src, first, last):
+            for q in range(4):
+                nc.tensor.matmul(
+                    bank[:, span(q, P)], lhsT=src[:, span(q, P)], rhs=ident[:],
+                    start=(first and q == 0), stop=(last and q == 3), is_transpose=True,
+                )
+
+        def bank_walk(bank):
+            return bank[:].rearrange("m (q p t) -> m p t q", q=4, t=PACK)
+
+        def turned_walk(ap):
+            return ap.rearrange("m (t p q) -> m p t q", q=4, t=PACK)
+
+        def plain_walk(ap):
+            return ap.rearrange("m (p t q) -> m p t q", q=4, t=PACK)
+
+        banks = [ring_bank() for h in range(HALVES)]
+        evidence_mm(0, banks)
+        for h in range(HALVES):
+            evidence_out(banks, slot_z, h)
+            scatter(page_b[0], idx3[:, span(h, LIST_COLS)], slot_z[:, span(h, BANK)], gain2[:, span(h, BANK)])
+
+        evidence_mm(1, lin_banks)
+        for a in range(PASSES):
+            cast_interleave(w1_bf[:, span(a, PACK * H)], w1_raw[a][:])
+        for a in range(PASSES):
+            nc.vector.quantize_mx(
+                out=w1_c[:, span(a, H)].bitcast(FP8X4), scales=w1_s[:, span(a, H)], in_=w1_bf[:, span(a, PACK * H)]
+            )
+        for h in range(HALVES):
+            evidence_out(lin_banks, slot_x, h)
+        scatter(page_b[1], idx3[:], slot_x[:, 0:S], gain2[:])
+
+        slot_h = sbuf("slot_h", 2 * S, F32, tag="stage1")
+        prior_neg01 = [sbuf("prior_neg%d" % c, T2, F32) for c in range(2)]
+        prior_neg23 = sbuf("prior_neg23", 2 * T2, F32, tag="big1")
+        prior_neg = [prior_neg01[0][:], prior_neg01[1][:], prior_neg23[:, 0:T2], prior_neg23[:, T2 : 2 * T2]]
+        z_bf = sbuf("z_bf", CHUNKS * BANK * PACK, BF16, tag="big0")
+        z_stage = sbuf("z_stage", 8 * BANK, BF16, tag="stage0")
+        claims = [slot_h, slot_y]
+        moved = [slot_y, slot_z]
+
+        def squares(c):
+            for h in range(HALVES):
+                bank = ring_bank()
+                project(bank, 2, c, h)
+                nc.scalar.activation(slot_h[:, S + h * BANK : S + (h + 1) * BANK], bank[:], SQUARE)
+
+        def linear(c):
+            for h in range(HALVES):
+                project(lin_banks[h], 1, c, h)
+
+        def claim_scatter(c):
+            dst = claims[c % 2]
+            for h in range(HALVES):
+                nc.vector.tensor_tensor(
+                    dst[:, span(h, BANK)], lin_banks[h][:], slot_h[:, S + h * BANK : S + (h + 1) * BANK], ADD
+                )
+            scatter(page_a[c % 2], idx2[:], dst[:, 0:S], gain1[:])
+
+        def turn_prior(c):
+            for g in range(CHUNKS):
+                bank = ring_bank()
+                turn(bank, prior_t[c][:, span(g, BANK)], True, True)
+                nc.scalar.activation(turned_walk(prior_neg[c][:, span(g, BANK)]), bank_walk(bank), COPY, scale=-1.0)
+
+        def gates(c):
+            for g in range(CHUNKS):
+                bank = ring_bank()
+                turn(bank, page_a[c % 2][:, span(g, BANK)], True, True)
+                nc.scalar.activation(plain_walk(gate_t[c % 2][:, span(g, BANK)]), bank_walk(bank), SIGMOID)
+
+        def diff_open(c, g):
+            turn(diff_banks[g], prior_t[c][:, span(g, BANK)], True, False)
+
+        def diff_close(c, g):
+            turn(diff_banks[g], page_b[c % 2][:, span(g, BANK)], False, True)
+
+        def diffs(c):
+            for g in range(CHUNKS):
+                diff_open(c, g)
+                diff_close(c, g)
+
+        def weigh(c, g):
+            nc.vector.tensor_tensor(
+                turned_walk(moved[c % 2][:, span(g, BANK)]), bank_walk(diff_banks[g]),
+                plain_walk(gate_t[c % 2][:, span(g, BANK)]), MULT,
+            )
+
+        def turn_back(c, g):
+            bank = ring_bank()
+            turn(bank, prior_neg[c][:, span(g, BANK)], True, False)
+            turn(bank, moved[c % 2][:, span(g, BANK)], False, True)
+            stage = z_stage[:, span((c * CHUNKS + g) % 8, BANK)]
+            nc.scalar.activation(
+                stage.rearrange("k (m t) -> k m t", t=PACK), bank[:].rearrange("k (t m) -> k m t", t=PACK),
+                COPY, scale=-1.0,
+            )
+            nc.sync.dma_start(
+                out=z_bf[32 * c : 32 * c + 32, span(g, BANK * PACK)].rearrange("p (q e) -> p q e", q=4),
+                in_=stage,
+            )
+
+        squares(0)
+        linear(0)
+        claim_scatter(0)
+        turn_prior(0)
+        diffs(0)
+        turn_prior(1)
+        squares(1)
+        linear(1)
+        claim_scatter(1)
+        turn_prior(2)
+        turn_prior(3)
+        cast_interleave(w4_bf[:], w4_raw[:])
+        for lo, hi in ((0, 256), (256, N)):
+            nc.vector.quantize_mx(
+                out=w4_c[:, lo:hi].bitcast(FP8X4), scales=w4_s[:, lo:hi], in_=w4_bf[:, PACK * lo : PACK * hi]
+            )
+        gates(0)
+        banks = [ring_bank() for h in range(HALVES)]
+        evidence_mm(2, banks)
+        for h in range(HALVES):
+            evidence_out(banks, slot_z, h)
+        squares(2)
+        linear(2)
+        for g in range(CHUNKS):
+            weigh(0, g)
+        scatter(page_b[0], idx3[:], slot_z[:, 0:S], gain2[:])
+        gates(1)
+        diffs(1)
+        for g in range(CHUNKS):
+            turn_back(0, g)
+        for g in range(CHUNKS):
+            weigh(1, g)
+        claim_scatter(2)
+        squares(3)
+        linear(3)
+        diffs(2)
+        gates(2)
+        for g in range(CHUNKS):
+            turn_back(1, g)
+        claim_scatter(3)
+        evidence_mm(3, lin_banks)
+        for h in range(HALVES):
+            evidence_out(lin_banks, slot_x, h)
+        for g in range(CHUNKS):
+            weigh(2, g)
+        scatter(page_b[1], idx3[:], slot_x[:, 0:S], gain2[:])
+        gates(3)
+        for g in range(CHUNKS):
+            diff_open(3, g)
+        for g in range(CHUNKS):
+            turn_back(2, g)
+
+        results = [sbuf("result%d" % i, T2, F32, tag="prior%d" % i) for i in range(2)]
+        for g in range(CHUNKS):
+            diff_close(3, g)
+            weigh(3, g)
+            turn_back(3, g)
+        for g in range(CHUNKS):
+            nc.vector.quantize_mx(out=z_c[g][:].bitcast(FP8X4), scales=z_s[g][:], in_=z_bf[:, span(g, BANK * PACK)])
+            for n in range(N // P):
+                bank = (lin_banks[0], lin_banks[1], diff_banks[g])[n]
+                nc.tensor.matmul_mx(
+                    out=bank[:], lhsT=w4_c[:, span(n, P)].bitcast(FP8X4), lhsT_scale=w4_s[:, span(n, P)],
+                    rhs=z_c[g][:].bitcast(FP8X4), rhs_scale=z_s[g][:], start=True, stop=True,
+                )
+                i = (g * (N // P) + n) % 8
+                result = results[i // 4][:, span(i % 4, BANK)]
+                if n == 1:
+                    nc.vector.tensor_copy(result, bank[:])
+                else:
+                    nc.scalar.copy(result, bank[:])
+                nc.sync.dma_start(out=out[span(n, P), span(g, BANK)], in_=result)

@@ -38,10 +38,14 @@ def tile_list_claim_evidence_desk_kernel(
     with ExitStack() as ctx:
         lists = ctx.enter_context(tc.tile_pool(name="lists", bufs=1))
         sb = ctx.enter_context(tc.tile_pool(name="sb", bufs=1))
+        shared = ctx.enter_context(tc.tile_pool(name="shared", bufs=1))
         ps = ctx.enter_context(tc.psum_pool(name="ps", bufs=1))
 
         def sbuf(name, cols, dtype, tag=None):
             return sb.tile([P, cols], dtype, name=name, tag=tag or name, align_bytes=64)
+
+        def placed(name, cols, dtype, offset):
+            return shared.tile([P, cols], dtype, name=name, align_bytes=64, offset=offset)
 
         def span(i, width):
             return slice(i * width, (i + 1) * width)
@@ -53,16 +57,9 @@ def tile_list_claim_evidence_desk_kernel(
         diff_banks = [ps.tile([P, BANK], F32, name="diff%d" % g) for g in range(CHUNKS)]
         lin_banks = [ps.tile([P, BANK], F32, name="lin%d" % h) for h in range(HALVES)]
         ring_banks = [ps.tile([P, BANK], F32, name="ring%d" % h) for h in range(2)]
-        ring_count = [0]
 
-        def ring_bank():
-            bank = ring_banks[ring_count[0] % 2]
-            ring_count[0] = ring_count[0] + 1
-            return bank
-
-        tab_w = [sbuf("tab_w%d" % a, T, I32, tag="big%d" % a) for a in range(PASSES)]
-        tab_s = sbuf("tab_s", T, U8)
-        got_w = [sbuf("got_w%d" % a, S, U32) for a in range(PASSES)]
+        tab_w = [placed("tab_w%d" % a, T, I32, a * 4 * T) for a in range(PASSES)]
+        tab_s = sbuf("tab_s", T, U8, tag="scales")
         got_s = sbuf("got_s", S, U8)
         got_s1 = sbuf("got_s1", S, U8)
         w1_raw0 = sbuf("w1_raw0", PACK * H, F32, tag="stage0")
@@ -82,28 +79,27 @@ def tile_list_claim_evidence_desk_kernel(
         gain1 = sbuf("gain1", S, F32)
         gain2 = sbuf("gain2", S, F32)
         prior_t = [sbuf("prior%d" % c, T2, F32, tag="prior%d" % c) for c in range(SLICES)]
-        page_a = [sbuf("page_a%d" % i, T2, F32) for i in range(2)]
-        page_b = [sbuf("page_b%d" % i, T2, F32) for i in range(2)]
-        gate_t = [sbuf("gate_t%d" % i, T2, F32) for i in range(2)]
+        page_b0 = sbuf("page_b0", T2, F32)
+        gate_t = [sbuf("gate_t0", T2 + BANK, F32), sbuf("gate_t1", T2, F32)]
+        slot_w = sbuf("slot_w", S, F32)
         slot_y = sbuf("slot_y", T2, F32)
         slot_z = sbuf("slot_z", T2, F32)
         ident = sbuf("ident", P, F32)
         z_c = [sbuf("z_c%d" % g, BANK, U32) for g in range(CHUNKS)]
         z_s = [sbuf("z_s%d" % g, BANK, U8) for g in range(CHUNKS)]
 
-        nc.vector.memset(tab_s[:].bitcast(I32), 0)
-        nc.vector.memset(w3_s[:].bitcast(I32), 0)
+        nc.gpsimd.memset(w3_s[:].bitcast(I32), 0)
+        nc.gpsimd.memset(tab_s[:].bitcast(I32), 0)
         nc.vector.memset(w2_s[:].bitcast(I32), 0)
         nc.vector.memset(got_s1[:].bitcast(I32), 0)
-        for page in (page_b[0], page_b[1], page_a[0], page_a[1]):
-            nc.vector.memset(page[:], 0.0)
-
-        nc.sync.dma_start(idx[:], offs)
+        nc.vector.memset(page_b0[:], 0.0)
         for q in range(4):
-            nc.sync.dma_start(
+            nc.gpsimd.dma_start(
                 out=tab_s[32 * q : 32 * q + 8, :].bitcast(I32),
                 in_=tab_scales[:, 4 * q : 4 * q + 4, :].bitcast(I32),
             )
+
+        nc.sync.dma_start(idx[:], offs)
         for a in range(PASSES):
             nc.sync.dma_start(out=tab_w[a][:], in_=tab_words[a].rearrange("p n t -> p (n t)").bitcast(I32))
         nc.sync.dma_start(
@@ -116,11 +112,6 @@ def tile_list_claim_evidence_desk_kernel(
                 in_=w3_scales[:, 4 * q : 4 * q + 4, :].bitcast(I32),
             )
         make_identity(nc, ident[:])
-        for q in range(4):
-            nc.gpsimd.dma_start(
-                out=w2_s[32 * q : 32 * q + 4, :].bitcast(I32).rearrange("r (a n) -> r a n", a=PASSES),
-                in_=w2_scales[:, 4 * q : 4 * q + 4, :].bitcast(I32).rearrange("a r n -> r a n"),
-            )
         nc.sync.dma_start(out=gain2[:], in_=wg2)
         nc.sync.dma_start(idx3[:], offs3)
         for a in range(PASSES):
@@ -132,6 +123,11 @@ def tile_list_claim_evidence_desk_kernel(
             out=w2_c[:].bitcast(I32).rearrange("p (a n) -> p a n", a=PASSES),
             in_=w2_words.rearrange("a p n -> p a n").bitcast(I32),
         )
+        for q in range(4):
+            nc.sync.dma_start(
+                out=w2_s[32 * q : 32 * q + 4, :].bitcast(I32).rearrange("r (a n) -> r a n", a=PASSES),
+                in_=w2_scales[:, 4 * q : 4 * q + 4, :].bitcast(I32).rearrange("a r n -> r a n"),
+            )
         nc.sync.dma_start(out=gain1[:], in_=wg1)
         nc.sync.dma_start(idx2[:], offs2)
         for c in range(SLICES):
@@ -139,6 +135,7 @@ def tile_list_claim_evidence_desk_kernel(
         nc.sync.dma_start(out=w4_raw[:], in_=w4.rearrange("(p j) n -> p (j n)", j=PACK))
 
         nc.vector.tensor_copy(got_s[:], tab_s[:].indirect(idx[:]))
+        got_w = [sbuf("got_w0", S, U32), sbuf("got_w1", S, U32, tag="scales")]
         for a in range(PASSES):
             for h in range(HALVES):
                 nc.vector.tensor_copy(
@@ -150,6 +147,11 @@ def tile_list_claim_evidence_desk_kernel(
                 out=got_s1[32 * q : 32 * q + 4, :].bitcast(I32),
                 in_=got_s[32 * q + 4 : 32 * q + 8, :].bitcast(I32),
             )
+
+        page_b = [page_b0, placed("page_b1", T2, F32, 4 * T)]
+        page_a = [placed("page_a0", T2, F32, 4 * T + 4 * T2)]
+        for page in (page_b[1], page_a[0]):
+            nc.gpsimd.memset(page[:], 0.0)
 
         def project(bank, which, c, h):
             for a in range(PASSES):
@@ -200,10 +202,9 @@ def tile_list_claim_evidence_desk_kernel(
         def plain_walk(ap):
             return ap.rearrange("m (p t q) -> m p t q", q=4, t=PACK)
 
-        banks = [ring_bank() for h in range(HALVES)]
-        evidence_mm(0, banks)
+        evidence_mm(0, lin_banks)
         for h in range(HALVES):
-            evidence_out(banks, slot_z, h)
+            evidence_out(lin_banks, slot_z, h)
             scatter(page_b[0], idx3[:, span(h, LIST_COLS)], slot_z[:, span(h, BANK)], gain2[:, span(h, BANK)])
 
         evidence_mm(1, lin_banks)
@@ -217,50 +218,60 @@ def tile_list_claim_evidence_desk_kernel(
             evidence_out(lin_banks, slot_x, h)
         scatter(page_b[1], idx3[:], slot_x[:, 0:S], gain2[:])
 
-        slot_h = sbuf("slot_h", 2 * S, F32, tag="stage1")
-        prior_neg01 = [sbuf("prior_neg%d" % c, T2, F32) for c in range(2)]
-        prior_neg23 = sbuf("prior_neg23", 2 * T2, F32, tag="big1")
-        prior_neg = [prior_neg01[0][:], prior_neg01[1][:], prior_neg23[:, 0:T2], prior_neg23[:, T2 : 2 * T2]]
-        z_bf = sbuf("z_bf", CHUNKS * BANK * PACK, BF16, tag="big0")
-        z_stage = sbuf("z_stage", 8 * BANK, BF16, tag="stage0")
-        claims = [slot_h, slot_y]
+        squared0 = sbuf("squared0", S, F32, tag="stage1")
+        squared1 = sbuf("squared1", S, F32)
+        squared2 = sbuf("squared2", S, F32)
+        squared = [squared0, squared1, squared2, squared1]
+        prior_neg = [sbuf("prior_neg%d" % c, T2, F32, tag="stage0" if c == 2 else None) for c in range(3)]
+        prior_neg.append(placed("prior_neg3", T2, F32, 0))
+        z_bf = sbuf("z_bf", CHUNKS * BANK * PACK, BF16)
+        z_stage = placed("z_stage", 8 * BANK, BF16, 4 * T2)
+        behind_gate = gate_t[0][:, T2 - BANK : T2 + BANK]
+        claims = [squared1[:, 0:S], slot_y[:, 0:S], gate_t[0][:, T2 - S : T2], behind_gate]
         moved = [slot_y, slot_z]
 
-        def squares(c):
+        def squares(c, banks):
             for h in range(HALVES):
-                bank = ring_bank()
-                project(bank, 2, c, h)
-                nc.scalar.activation(slot_h[:, S + h * BANK : S + (h + 1) * BANK], bank[:], SQUARE)
+                project(banks[h], 2, c, h)
+                nc.scalar.activation(squared[c][:, span(h, BANK)], banks[h][:], SQUARE)
 
-        def linear(c):
+        def linear(c, banks):
             for h in range(HALVES):
-                project(lin_banks[h], 1, c, h)
+                project(banks[h], 1, c, h)
+
+        def claim_sum(c, h, banks):
+            nc.vector.tensor_tensor(claims[c][:, span(h, BANK)], banks[h][:], squared[c][:, span(h, BANK)], ADD)
 
         def claim_scatter(c):
-            dst = claims[c % 2]
-            for h in range(HALVES):
-                nc.vector.tensor_tensor(
-                    dst[:, span(h, BANK)], lin_banks[h][:], slot_h[:, S + h * BANK : S + (h + 1) * BANK], ADD
-                )
-            scatter(page_a[c % 2], idx2[:], dst[:, 0:S], gain1[:])
+            scatter(page_a[c % 2], idx2[:], claims[c], gain1[:])
 
-        def turn_prior(c):
+        def weighs(c):
             for g in range(CHUNKS):
-                bank = ring_bank()
+                weigh(c, g)
+
+        def turn_prior(c, banks):
+            for g in range(CHUNKS):
+                bank = banks[g]
                 turn(bank, prior_t[c][:, span(g, BANK)], True, True)
                 nc.scalar.activation(turned_walk(prior_neg[c][:, span(g, BANK)]), bank_walk(bank), COPY, scale=-1.0)
 
-        def gates(c):
+        def gate(c, g, bank):
+            turn(bank, page_a[c % 2][:, span(g, BANK)], True, True)
+            nc.scalar.activation(plain_walk(gate_t[c % 2][:, span(g, BANK)]), bank_walk(bank), SIGMOID)
+
+        def next_slice(c):
             for g in range(CHUNKS):
-                bank = ring_bank()
-                turn(bank, page_a[c % 2][:, span(g, BANK)], True, True)
-                nc.scalar.activation(plain_walk(gate_t[c % 2][:, span(g, BANK)]), bank_walk(bank), SIGMOID)
+                gate(c, g, diff_banks[g])
+            for g in range(CHUNKS):
+                turn_back(c - 1, g, diff_banks[g])
+            for g in range(CHUNKS):
+                diff_open(c, g)
 
         def diff_open(c, g):
             turn(diff_banks[g], prior_t[c][:, span(g, BANK)], True, False)
 
         def diff_close(c, g):
-            turn(diff_banks[g], page_b[c % 2][:, span(g, BANK)], False, True)
+            turn(diff_banks[g], page_b[(0, 1, 1, 0)[c]][:, span(g, BANK)], False, True)
 
         def diffs(c):
             for g in range(CHUNKS):
@@ -273,9 +284,14 @@ def tile_list_claim_evidence_desk_kernel(
                 plain_walk(gate_t[c % 2][:, span(g, BANK)]), MULT,
             )
 
-        def turn_back(c, g):
-            bank = ring_bank()
+        def back_open(c, g, bank):
             turn(bank, prior_neg[c][:, span(g, BANK)], True, False)
+
+        def turn_back(c, g, bank):
+            back_open(c, g, bank)
+            back_close(c, g, bank)
+
+        def back_close(c, g, bank):
             turn(bank, moved[c % 2][:, span(g, BANK)], False, True)
             stage = z_stage[:, span((c * CHUNKS + g) % 8, BANK)]
             nc.scalar.activation(
@@ -287,72 +303,88 @@ def tile_list_claim_evidence_desk_kernel(
                 in_=stage,
             )
 
-        squares(0)
-        linear(0)
+        def evidence(c, banks, dst):
+            evidence_mm(c, banks)
+            for h in range(HALVES):
+                evidence_out(banks, dst, h)
+
+        squares(0, ring_banks)
+        linear(0, lin_banks)
+        squares(1, ring_banks)
+        linear(1, ring_banks)
+        for h in range(HALVES):
+            claim_sum(1, h, ring_banks)
+        for h in range(HALVES):
+            claim_sum(0, h, lin_banks)
         claim_scatter(0)
-        turn_prior(0)
-        diffs(0)
-        turn_prior(1)
-        squares(1)
-        linear(1)
+        page_a.append(sbuf("page_a1", T2, F32, tag="stage1"))
+        nc.gpsimd.memset(page_a[1][:], 0.0)
         claim_scatter(1)
-        turn_prior(2)
-        turn_prior(3)
+        turn_prior(0, diff_banks[2:] * 2)
+        for g in (0, 1):
+            diff_open(0, g)
+            diff_close(0, g)
+        turn_prior(1, diff_banks[2:] * 2)
+        linear(2, lin_banks)
+        turn_prior(2, ring_banks * 2)
+        turn_prior(3, ring_banks + diff_banks[2:])
+        squares(2, ring_banks)
         cast_interleave(w4_bf[:], w4_raw[:])
         for lo, hi in ((0, 256), (256, N)):
             nc.vector.quantize_mx(
                 out=w4_c[:, lo:hi].bitcast(FP8X4), scales=w4_s[:, lo:hi], in_=w4_bf[:, PACK * lo : PACK * hi]
             )
-        gates(0)
-        banks = [ring_bank() for h in range(HALVES)]
-        evidence_mm(2, banks)
+        for g in (2, 3, 0, 1):
+            gate(0, g, (ring_banks + diff_banks[2:])[g])
+        for g in (2, 3):
+            diff_open(0, g)
+            diff_close(0, g)
+        weighs(0)
         for h in range(HALVES):
-            evidence_out(banks, slot_z, h)
-        squares(2)
-        linear(2)
-        for g in range(CHUNKS):
-            weigh(0, g)
-        scatter(page_b[0], idx3[:], slot_z[:, 0:S], gain2[:])
-        gates(1)
-        diffs(1)
-        for g in range(CHUNKS):
-            turn_back(0, g)
-        for g in range(CHUNKS):
-            weigh(1, g)
+            claim_sum(2, h, lin_banks)
         claim_scatter(2)
-        squares(3)
-        linear(3)
-        diffs(2)
-        gates(2)
+        evidence(2, diff_banks, slot_w)
+        next_slice(1)
         for g in range(CHUNKS):
-            turn_back(1, g)
+            diff_close(1, g)
+        linear(3, lin_banks)
+        weighs(1)
+        scatter(page_b[1], idx3[:], slot_w[:], gain2[:])
+        squares(3, diff_banks)
+        next_slice(2)
+        for g in range(CHUNKS):
+            diff_close(2, g)
+        claim_sum(3, 1, lin_banks)
+        weighs(2)
+        claim_sum(3, 0, lin_banks)
         claim_scatter(3)
-        evidence_mm(3, lin_banks)
-        for h in range(HALVES):
-            evidence_out(lin_banks, slot_x, h)
+        evidence(3, lin_banks, slot_x)
+        scatter(page_b[0], idx3[:], slot_x[:, 0:S], gain2[:])
         for g in range(CHUNKS):
-            weigh(2, g)
-        scatter(page_b[1], idx3[:], slot_x[:, 0:S], gain2[:])
-        gates(3)
+            turn_back(2, g, diff_banks[g])
+        last_banks = ring_banks + lin_banks
+        for g in range(CHUNKS):
+            back_open(3, g, last_banks[g])
+        for g in range(CHUNKS):
+            gate(3, g, diff_banks[g])
         for g in range(CHUNKS):
             diff_open(3, g)
-        for g in range(CHUNKS):
-            turn_back(2, g)
 
         results = [sbuf("result%d" % i, T2, F32, tag="prior%d" % i) for i in range(2)]
+        out_banks = diff_banks + last_banks
         for g in range(CHUNKS):
             diff_close(3, g)
             weigh(3, g)
-            turn_back(3, g)
+            back_close(3, g, last_banks[g])
         for g in range(CHUNKS):
             nc.vector.quantize_mx(out=z_c[g][:].bitcast(FP8X4), scales=z_s[g][:], in_=z_bf[:, span(g, BANK * PACK)])
             for n in range(N // P):
-                bank = (lin_banks[0], lin_banks[1], diff_banks[g])[n]
+                i = (g * (N // P) + n) % 8
+                bank = out_banks[i]
                 nc.tensor.matmul_mx(
                     out=bank[:], lhsT=w4_c[:, span(n, P)].bitcast(FP8X4), lhsT_scale=w4_s[:, span(n, P)],
                     rhs=z_c[g][:].bitcast(FP8X4), rhs_scale=z_s[g][:], start=True, stop=True,
                 )
-                i = (g * (N // P) + n) % 8
                 result = results[i // 4][:, span(i % 4, BANK)]
                 if n == 1:
                     nc.vector.tensor_copy(result, bank[:])

from contextlib import ExitStack

import concourse.mybir as mybir
from concourse.masks import make_identity

K, T, S, H, T2, N = 1024, 4096, 1024, 512, 2048, 384
FLOPS = 3 * 2 * K * H * S + 2 * H * N * T2

F32 = mybir.dt.float32
BF16 = mybir.dt.bfloat16
I32 = mybir.dt.int32
U32 = mybir.dt.uint32
U16 = mybir.dt.uint16
U8 = mybir.dt.uint8
FP8X4 = mybir.dt.float8_e4m3fn_x4
FP4X4 = mybir.dt.float4_e2m1fn_x4
MULT = mybir.AluOpType.mult
ADD = mybir.AluOpType.add
COPY = mybir.ActivationFunctionType.Copy
SQUARE = mybir.ActivationFunctionType.Square
SIGMOID = mybir.ActivationFunctionType.Sigmoid

P = 128
PACK = 4
BANK = 512
PASSES = K // (P * PACK)
SLICES = H // P
CHUNKS = T2 // BANK
HALVES = S // BANK
LIST_COLS = BANK // 16


def tile_list_claim_evidence_desk_kernel(
    tc, tab_words, tab_scales, offs, w1, w2_words, w2_scales, w3_words, w3_scales,
    offs2, wg1, offs3, wg2, prior, w4, out,
):
    nc = tc.nc
    with ExitStack() as ctx:
        lists = ctx.enter_context(tc.tile_pool(name="lists", bufs=1))
        sb = ctx.enter_context(tc.tile_pool(name="sb", bufs=1))
        shared = ctx.enter_context(tc.tile_pool(name="shared", bufs=1))
        ps = ctx.enter_context(tc.psum_pool(name="ps", bufs=1))

        def sbuf(name, cols, dtype, tag=None):
            return sb.tile([P, cols], dtype, name=name, tag=tag or name, align_bytes=64)

        def placed(name, cols, dtype, offset):
            return shared.tile([P, cols], dtype, name=name, align_bytes=64, offset=offset)

        def span(i, width):
            return slice(i * width, (i + 1) * width)

        idx = lists.tile([P, S // 16], U16, name="idx")
        idx2 = lists.tile([P, S // 16], U16, name="idx2")
        idx3 = lists.tile([P, S // 16], U16, name="idx3")

        diff_banks = [ps.tile([P, BANK], F32, name="diff%d" % g) for g in range(CHUNKS)]
        lin_banks = [ps.tile([P, BANK], F32, name="lin%d" % h) for h in range(HALVES)]
        ring_banks = [ps.tile([P, BANK], F32, name="ring%d" % h) for h in range(2)]

        tab_w = [placed("tab_w%d" % a, T, I32, a * 4 * T) for a in range(PASSES)]
        tab_s = sbuf("tab_s", T, U8, tag="scales")
        got_s = sbuf("got_s", S, U8)
        got_s1 = sbuf("got_s1", S, U8)
        w1_raw0 = sbuf("w1_raw0", PACK * H, F32, tag="stage0")
        slot_x = sbuf("slot_x", PACK * H, F32)
        w1_raw = [w1_raw0, slot_x]
        w1_bf = sbuf("w1_bf", PASSES * PACK * H, BF16, tag="stage1")
        w1_c = sbuf("w1_c", PASSES * H, U32)
        w1_s = sbuf("w1_s", PASSES * H, U8)
        w2_c = sbuf("w2_c", PASSES * 2 * H, U8)
        w2_s = sbuf("w2_s", PASSES * H, U8)
        w3_c = sbuf("w3_c", PASSES * H, I32)
        w3_s = sbuf("w3_s", H, U8)
        w4_raw = sbuf("w4_raw", PACK * N, F32)
        w4_bf = sbuf("w4_bf", PACK * N, BF16)
        w4_c = sbuf("w4_c", N, U32)
        w4_s = sbuf("w4_s", N, U8)
        gain1 = sbuf("gain1", S, F32)
        gain2 = sbuf("gain2", S, F32)
        prior_t = [sbuf("prior%d" % c, T2, F32, tag="prior%d" % c) for c in range(SLICES)]
        page_b0 = sbuf("page_b0", T2, F32)
        gate_t = [sbuf("gate_t0", T2 + BANK, F32), sbuf("gate_t1", T2, F32)]
        slot_w = sbuf("slot_w", S, F32)
        slot_y = sbuf("slot_y", T2, F32)
        slot_z = sbuf("slot_z", T2, F32)
        ident = sbuf("ident", P, F32)
        z_c = [sbuf("z_c%d" % g, BANK, U32) for g in range(CHUNKS)]
        z_s = [sbuf("z_s%d" % g, BANK, U8) for g in range(CHUNKS)]

        nc.gpsimd.memset(w3_s[:].bitcast(I32), 0)
        nc.gpsimd.memset(tab_s[:].bitcast(I32), 0)
        nc.vector.memset(w2_s[:].bitcast(I32), 0)
        nc.vector.memset(got_s1[:].bitcast(I32), 0)
        nc.vector.memset(page_b0[:], 0.0)
        for q in range(4):
            nc.gpsimd.dma_start(
                out=tab_s[32 * q : 32 * q + 8, :].bitcast(I32),
                in_=tab_scales[:, 4 * q : 4 * q + 4, :].bitcast(I32),
            )

        nc.sync.dma_start(idx[:], offs)
        for a in range(PASSES):
            nc.sync.dma_start(out=tab_w[a][:], in_=tab_words[a].rearrange("p n t -> p (n t)").bitcast(I32))
        nc.sync.dma_start(
            out=w3_c[:].rearrange("p (a n) -> p a n", a=PASSES),
            in_=w3_words.rearrange("a p n t -> p a (n t)").bitcast(I32),
        )
        for q in range(4):
            nc.sync.dma_start(
                out=w3_s[32 * q : 32 * q + 8, :].bitcast(I32),
                in_=w3_scales[:, 4 * q : 4 * q + 4, :].bitcast(I32),
            )
        make_identity(nc, ident[:])
        nc.sync.dma_start(out=gain2[:], in_=wg2)
        nc.sync.dma_start(idx3[:], offs3)
        for a in range(PASSES):
            nc.sync.dma_start(
                out=w1_raw[a][:],
                in_=w1[span(a, P * PACK), :].rearrange("(p j) n -> p (j n)", j=PACK),
            )
        nc.sync.dma_start(
            out=w2_c[:].bitcast(I32).rearrange("p (a n) -> p a n", a=PASSES),
            in_=w2_words.rearrange("a p n -> p a n").bitcast(I32),
        )
        for q in range(4):
            nc.sync.dma_start(
                out=w2_s[32 * q : 32 * q + 4, :].bitcast(I32).rearrange("r (a n) -> r a n", a=PASSES),
                in_=w2_scales[:, 4 * q : 4 * q + 4, :].bitcast(I32).rearrange("a r n -> r a n"),
            )
        nc.sync.dma_start(out=gain1[:], in_=wg1)
        nc.sync.dma_start(idx2[:], offs2)
        for c in range(SLICES):
            nc.sync.dma_start(out=prior_t[c][:], in_=prior[span(c, P), :])
        nc.sync.dma_start(out=w4_raw[:], in_=w4.rearrange("(p j) n -> p (j n)", j=PACK))

        nc.vector.tensor_copy(got_s[:], tab_s[:].indirect(idx[:]))
        got_w = [sbuf("got_w0", S, U32), sbuf("got_w1", S, U32, tag="scales")]
        for a in range(PASSES):
            for h in range(HALVES):
                nc.vector.tensor_copy(
                    got_w[a][:, span(h, BANK)],
                    tab_w[a][:].bitcast(U32).indirect(idx[:, span(h, LIST_COLS)]),
                )
        for q in range(4):
            nc.gpsimd.dma_start(
                out=got_s1[32 * q : 32 * q + 4, :].bitcast(I32),
                in_=got_s[32 * q + 4 : 32 * q + 8, :].bitcast(I32),
            )

        page_b = [page_b0, placed("page_b1", T2, F32, 4 * T)]
        page_a = [placed("page_a0", T2, F32, 4 * T + 4 * T2)]
        for page in (page_b[1], page_a[0]):
            nc.gpsimd.memset(page[:], 0.0)

        def project(bank, which, c, h):
            for a in range(PASSES):
                cols = slice(a * H + c * P, a * H + (c + 1) * P)
                if which == 1:
                    lhs, lhs_s, rhs_s = w1_c[:, cols].bitcast(FP8X4), w1_s[:, cols], got_s[4 * a : P, span(h, BANK)]
                elif which == 2:
                    lhs = w2_c[:, 2 * cols.start : 2 * cols.stop].bitcast(FP4X4)
                    lhs_s, rhs_s = w2_s[:, cols], (got_s, got_s1)[a][:, span(h, BANK)]
                else:
                    lhs, lhs_s = w3_c[:, cols].bitcast(FP8X4), w3_s[4 * a : P, span(c, P)]
                    rhs_s = got_s[4 * a : P, span(h, BANK)]
                nc.tensor.matmul_mx(
                    out=bank[:], lhsT=lhs, lhsT_scale=lhs_s,
                    rhs=got_w[a][:, span(h, BANK)].bitcast(FP8X4), rhs_scale=rhs_s,
                    start=(a == 0), stop=(a == PASSES - 1),
                )

        def cast_interleave(dst, src):
            nc.scalar.copy(
                out=dst.rearrange("p (c i t) -> p c t i", i=4, t=PACK),
                in_=src.rearrange("p (t c i) -> p c t i", i=4, t=PACK),
            )

        def evidence_mm(c, banks):
            for h in range(HALVES):
                project(banks[h], 3, c, h)

        def evidence_out(banks, dst, h):
            nc.scalar.activation(dst[:, span(h, BANK)], banks[h][:], COPY, scale=-1.0)

        def scatter(page, offsets, values, gain):
            nc.vector.tensor_tensor(page[:].indirect(offsets), values, gain, MULT)

        def turn(bank, src, first, last):
            for q in range(4):
                nc.tensor.matmul(
                    bank[:, span(q, P)], lhsT=src[:, span(q, P)], rhs=ident[:],
                    start=(first and q == 0), stop=(last and q == 3), is_transpose=True,
                )

        def bank_walk(bank):
            return bank[:].rearrange("m (q p t) -> m p t q", q=4, t=PACK)

        def turned_walk(ap):
            return ap.rearrange("m (t p q) -> m p t q", q=4, t=PACK)

        def plain_walk(ap):
            return ap.rearrange("m (p t q) -> m p t q", q=4, t=PACK)

        evidence_mm(0, lin_banks)
        for h in range(HALVES):
            evidence_out(lin_banks, slot_z, h)
            scatter(page_b[0], idx3[:, span(h, LIST_COLS)], slot_z[:, span(h, BANK)], gain2[:, span(h, BANK)])

        evidence_mm(1, lin_banks)
        for a in range(PASSES):
            cast_interleave(w1_bf[:, span(a, PACK * H)], w1_raw[a][:])
        for a in range(PASSES):
            nc.vector.quantize_mx(
                out=w1_c[:, span(a, H)].bitcast(FP8X4), scales=w1_s[:, span(a, H)], in_=w1_bf[:, span(a, PACK * H)]
            )
        for h in range(HALVES):
            evidence_out(lin_banks, slot_x, h)
        scatter(page_b[1], idx3[:], slot_x[:, 0:S], gain2[:])

        squared0 = sbuf("squared0", S, F32, tag="stage1")
        squared1 = sbuf("squared1", S, F32)
        squared2 = sbuf("squared2", S, F32)
        squared = [squared0, squared1, squared2, squared1]
        prior_neg = [sbuf("prior_neg%d" % c, T2, F32, tag="stage0" if c == 2 else None) for c in range(3)]
        prior_neg.append(placed("prior_neg3", T2, F32, 0))
        z_bf = sbuf("z_bf", CHUNKS * BANK * PACK, BF16)
        z_stage = placed("z_stage", 8 * BANK, BF16, 4 * T2)
        behind_gate = gate_t[0][:, T2 - BANK : T2 + BANK]
        claims = [squared1[:, 0:S], slot_y[:, 0:S], gate_t[0][:, T2 - S : T2], behind_gate]
        moved = [slot_y, slot_z]

        def squares(c, banks):
            for h in range(HALVES):
                project(banks[h], 2, c, h)
                nc.scalar.activation(squared[c][:, span(h, BANK)], banks[h][:], SQUARE)

        def linear(c, banks):
            for h in range(HALVES):
                project(banks[h], 1, c, h)

        def claim_sum(c, h, banks):
            nc.vector.tensor_tensor(claims[c][:, span(h, BANK)], banks[h][:], squared[c][:, span(h, BANK)], ADD)

        def claim_scatter(c):
            scatter(page_a[c % 2], idx2[:], claims[c], gain1[:])

        def weighs(c):
            for g in range(CHUNKS):
                weigh(c, g)

        def turn_prior(c, banks):
            for g in range(CHUNKS):
                bank = banks[g]
                turn(bank, prior_t[c][:, span(g, BANK)], True, True)
                nc.scalar.activation(turned_walk(prior_neg[c][:, span(g, BANK)]), bank_walk(bank), COPY, scale=-1.0)

        def gate(c, g, bank):
            turn(bank, page_a[c % 2][:, span(g, BANK)], True, True)
            nc.scalar.activation(plain_walk(gate_t[c % 2][:, span(g, BANK)]), bank_walk(bank), SIGMOID)

        def next_slice(c):
            for g in range(CHUNKS):
                gate(c, g, diff_banks[g])
            for g in range(CHUNKS):
                turn_back(c - 1, g, diff_banks[g])
            for g in range(CHUNKS):
                diff_open(c, g)

        def diff_open(c, g):
            turn(diff_banks[g], prior_t[c][:, span(g, BANK)], True, False)

        def diff_close(c, g):
            turn(diff_banks[g], page_b[(0, 1, 1, 0)[c]][:, span(g, BANK)], False, True)

        def diffs(c):
            for g in range(CHUNKS):
                diff_open(c, g)
                diff_close(c, g)

        def weigh(c, g):
            nc.vector.tensor_tensor(
                turned_walk(moved[c % 2][:, span(g, BANK)]), bank_walk(diff_banks[g]),
                plain_walk(gate_t[c % 2][:, span(g, BANK)]), MULT,
            )

        def back_open(c, g, bank):
            turn(bank, prior_neg[c][:, span(g, BANK)], True, False)

        def turn_back(c, g, bank):
            back_open(c, g, bank)
            back_close(c, g, bank)

        def back_close(c, g, bank):
            turn(bank, moved[c % 2][:, span(g, BANK)], False, True)
            stage = z_stage[:, span((c * CHUNKS + g) % 8, BANK)]
            nc.scalar.activation(
                stage.rearrange("k (m t) -> k m t", t=PACK), bank[:].rearrange("k (t m) -> k m t", t=PACK),
                COPY, scale=-1.0,
            )
            nc.sync.dma_start(
                out=z_bf[32 * c : 32 * c + 32, span(g, BANK * PACK)].rearrange("p (q e) -> p q e", q=4),
                in_=stage,
            )

        def evidence(c, banks, dst):
            evidence_mm(c, banks)
            for h in range(HALVES):
                evidence_out(banks, dst, h)

        squares(0, ring_banks)
        linear(0, lin_banks)
        squares(1, ring_banks)
        linear(1, ring_banks)
        for h in range(HALVES):
            claim_sum(1, h, ring_banks)
        for h in range(HALVES):
            claim_sum(0, h, lin_banks)
        claim_scatter(0)
        page_a.append(sbuf("page_a1", T2, F32, tag="stage1"))
        nc.gpsimd.memset(page_a[1][:], 0.0)
        claim_scatter(1)
        turn_prior(0, diff_banks[2:] * 2)
        for g in (0, 1):
            diff_open(0, g)
            diff_close(0, g)
        turn_prior(1, diff_banks[2:] * 2)
        linear(2, lin_banks)
        turn_prior(2, ring_banks * 2)
        turn_prior(3, ring_banks + diff_banks[2:])
        squares(2, ring_banks)
        cast_interleave(w4_bf[:], w4_raw[:])
        for lo, hi in ((0, 256), (256, N)):
            nc.vector.quantize_mx(
                out=w4_c[:, lo:hi].bitcast(FP8X4), scales=w4_s[:, lo:hi], in_=w4_bf[:, PACK * lo : PACK * hi]
            )
        for g in (2, 3, 0, 1):
            gate(0, g, (ring_banks + diff_banks[2:])[g])
        for g in (2, 3):
            diff_open(0, g)
            diff_close(0, g)
        weighs(0)
        for h in range(HALVES):
            claim_sum(2, h, lin_banks)
        claim_scatter(2)
        evidence(2, diff_banks, slot_w)
        next_slice(1)
        for g in range(CHUNKS):
            diff_close(1, g)
        linear(3, lin_banks)
        weighs(1)
        scatter(page_b[1], idx3[:], slot_w[:], gain2[:])
        squares(3, diff_banks)
        next_slice(2)
        for g in range(CHUNKS):
            diff_close(2, g)
        claim_sum(3, 1, lin_banks)
        weighs(2)
        claim_sum(3, 0, lin_banks)
        claim_scatter(3)
        evidence(3, lin_banks, slot_x)
        scatter(page_b[0], idx3[:], slot_x[:, 0:S], gain2[:])
        for g in range(CHUNKS):
            turn_back(2, g, diff_banks[g])
        last_banks = ring_banks + lin_banks
        for g in range(CHUNKS):
            back_open(3, g, last_banks[g])
        for g in range(CHUNKS):
            gate(3, g, diff_banks[g])
        for g in range(CHUNKS):
            diff_open(3, g)

        results = [sbuf("result%d" % i, T2, F32, tag="prior%d" % i) for i in range(2)]
        out_banks = diff_banks + last_banks
        for g in range(CHUNKS):
            diff_close(3, g)
            weigh(3, g)
            back_close(3, g, last_banks[g])
        for g in range(CHUNKS):
            nc.vector.quantize_mx(out=z_c[g][:].bitcast(FP8X4), scales=z_s[g][:], in_=z_bf[:, span(g, BANK * PACK)])
            for n in range(N // P):
                i = (g * (N // P) + n) % 8
                bank = out_banks[i]
                nc.tensor.matmul_mx(
                    out=bank[:], lhsT=w4_c[:, span(n, P)].bitcast(FP8X4), lhsT_scale=w4_s[:, span(n, P)],
                    rhs=z_c[g][:].bitcast(FP8X4), rhs_scale=z_s[g][:], start=True, stop=True,
                )
                result = results[i // 4][:, span(i % 4, BANK)]
                if n == 1:
                    nc.vector.tensor_copy(result, bank[:])
                else:
                    nc.scalar.copy(result, bank[:])
                nc.sync.dma_start(out=out[span(n, P), span(g, BANK)], in_=result)
